import numpy as np
import ml_dtypes


def mxq(x, axis, fmt="e4m3"):
    dtype, down = {"e4m3": (ml_dtypes.float8_e4m3fn, 7), "e5m2": (ml_dtypes.float8_e5m2, 14)}[fmt]
    v = np.moveaxis(np.asarray(x, np.float32).astype(ml_dtypes.bfloat16).astype(np.float64), axis, -1)
    blocks = v.reshape(v.shape[:-1] + (-1, 32))
    amax = np.abs(blocks).max(-1, keepdims=True)
    byte = np.maximum(np.where(amax > 0, np.frexp(amax)[1] - 1 + 127, 0) - down, 1)
    scale = np.exp2(byte - 127.0)
    codes = (blocks / scale).astype(np.float32).astype(dtype).astype(np.float64)
    return np.moveaxis((codes * scale).reshape(v.shape), -1, axis)


WIDE = False


def mx_kscale(k):
    if not WIDE:
        return np.ones(k)
    levels = np.array([10, -10, 5, -5, 0])
    if k % 512:
        return np.exp2(np.random.permutation(np.resize(levels, k // 32))).repeat(32)
    a = np.empty((k // 512, 16))
    for p in range(k // 512):
        a[p, :8] = np.random.permutation(np.resize(levels, 8))
        for g in range(8):
            far = levels[np.abs(levels - a[p, g]) >= 10]
            a[p, g + 8] = far[np.random.randint(len(far))]
    return np.exp2(a.ravel()).repeat(32)


def f64(x):
    return np.asarray(x).astype(np.float64)


def striped(idx):
    return np.tile(np.asarray(idx).reshape(-1, 16).T, (8, 1)).astype(np.uint16)


def unstriped(offs):
    return offs[:16].T.reshape(-1).astype(np.int64)


E2M1 = np.array([0.0, 0.5, 1.0, 1.5, 2.0, 3.0, 4.0, 6.0, -0.0, -0.5, -1.0, -1.5, -2.0, -3.0, -4.0, -6.0])


def pack_weight(w, fmt):
    k, n = w.shape
    w = f64(np.asarray(w, np.float32).astype(ml_dtypes.bfloat16)).reshape(k // 32, 32, n)
    amax = np.abs(w).max(1)
    if fmt == "e4m3":
        byte = np.frexp(amax)[1] - 1 + 127 - 7
    else:
        mant, ex = np.frexp(amax / 6.0)
        byte = np.where(mant > 0.5, ex, ex - 1) + 127
    byte = np.clip(np.where(amax > 0, byte, 1), 1, 254)
    scaled = (w * np.exp2(127.0 - byte)[:, None, :]).reshape(k, n).astype(np.float32)
    by_word = np.ascontiguousarray(scaled.reshape(k // 512, 128, 4, n).transpose(0, 1, 3, 2))
    if fmt == "e4m3":
        words = by_word.astype(ml_dtypes.float8_e4m3fn).view(np.uint8)
    else:
        c = by_word.astype(ml_dtypes.float4_e2m1fn).view(np.uint8) & 0xF
        words = (c[..., 0::2] | (c[..., 1::2] << 4)).reshape(k // 512, 128, 2 * n)
    return np.ascontiguousarray(words), np.ascontiguousarray(byte.astype(np.uint8).reshape(k // 512, 16, n))


def unpack_weight(words, scales, fmt):
    g, _, n = scales.shape
    words = np.ascontiguousarray(words).reshape(g, 128, n, -1)
    if fmt == "e4m3":
        vals = words.view(ml_dtypes.float8_e4m3fn).astype(np.float64)
    else:
        nib = np.empty((g, 128, n, 4), np.uint8)
        nib[..., 0::2] = words & 0xF
        nib[..., 1::2] = words >> 4
        vals = E2M1[nib]
    vals = vals * np.repeat(np.exp2(scales.astype(np.float64) - 127.0), 8, axis=1)[..., None]
    return vals.transpose(0, 1, 3, 2).reshape(g * 512, n)


def sigmoid(v):
    return 1.0 / (1.0 + np.exp(-v))


D, T, I, Q, U, M = 512, 2048, 512, 128, 1024, 2048


def setup_inputs():
    n = np.random.standard_normal
    idx = np.random.permutation(T)[:I]
    idx2 = np.random.permutation(U)[:Q]
    idx3 = np.random.permutation(U)[:Q]
    idx4 = np.random.permutation(M)[:I]
    fd = mx_kscale(D)
    keysp = pack_weight(n((D, T)) / fd[:, None], "e2m1")
    return {
        "users": (n((D, U)) * 1.0 / np.sqrt(D) * fd[:, None]).astype(np.float32),
        "keys_words": keysp[0],
        "keys_scales": keysp[1],
        "old": (np.random.uniform(0.0, 2.0, (Q, M))).astype(np.float32),
        "fade": (np.random.uniform(0.3, 0.9, (Q, 1))).astype(np.float32),
        "offs": striped(idx),
        "offs2": striped(idx2),
        "offs3": striped(idx3),
        "offs4": striped(idx4),
    }


def reference(users, keys_words, keys_scales, old, fade, offs, offs2, offs3, offs4):
    idx = unstriped(offs)
    idx2 = unstriped(offs2)
    idx3 = unstriped(offs3)
    idx4 = unstriped(offs4)
    keysu = unpack_weight(keys_words, keys_scales, "e2m1")
    zq = np.maximum(f64(users)[:, idx2], f64(users)[:, idx3])
    zqq = mxq(zq, 0, "e4m3")
    keysidxg = keysu[:, idx]
    s = zqq.T @ keysidxg
    w = sigmoid(s)
    ws = w * 2.0
    wf = np.zeros((Q, M))
    wf[:, idx4] = ws
    y = f64(old) * f64(fade) + wf
    return y

@@ -1,0 +1,124 @@
+import concourse.mybir as mybir
+
+F32 = mybir.dt.float32
+BF16 = mybir.dt.bfloat16
+I32 = mybir.dt.int32
+U32 = mybir.dt.uint32
+U16 = mybir.dt.uint16
+U8 = mybir.dt.uint8
+FP8X4 = mybir.dt.float8_e4m3fn_x4
+FP4X4 = mybir.dt.float4_e2m1fn_x4
+ALU = mybir.AluOpType
+ACT = mybir.ActivationFunctionType
+
+D, T, I, Q, U, M = 512, 2048, 512, 128, 1024, 2048
+P = 128
+PACK = 4
+LANES = 16
+HALF = I // 2
+OUT_CHUNKS = (512, 512, 512, 256, 256)
+
+FLOPS = 2 * D * Q * I
+
+
+def tile_attend_querylarger_counts_lean_kernel(tc, users, keys_words, keys_scales, old, fade, offs, offs2, offs3, offs4, out):
+    nc = tc.nc
+    with (
+        tc.tile_pool(name="lists", bufs=1) as lists,
+        tc.tile_pool(name="held", bufs=1) as held,
+        tc.psum_pool(name="psum", bufs=1) as psum,
+    ):
+        key_list = lists.tile([P, I // LANES], U16, name="key_list")
+        first_list = lists.tile([P, Q // LANES], U16, name="first_list")
+        second_list = lists.tile([P, Q // LANES], U16, name="second_list")
+        place_list = lists.tile([P, I // LANES], U16, name="place_list")
+
+        scale_pool = held.tile([P, T], U8, name="scale_pool")
+        nc.vector.memset(scale_pool[:].bitcast(I32), 0)
+
+        nc.sync.dma_start(first_list[:], offs2)
+        nc.sync.dma_start(second_list[:], offs3)
+        nc.sync.dma_start(key_list[:], offs)
+
+        planes = users.rearrange("(p t) u -> p t u", t=PACK)
+        users012 = held.tile([P, 3, U], F32, name="users012", tag="slot_a")
+        users3 = held.tile([P, U], F32, name="users3", tag="slot_b")
+        word_pool = held.tile([P, T], U16, name="word_pool", tag="slot_c")
+        nc.sync.dma_start(users012[:], planes[:, 0:3, :])
+        for quad in range(4):
+            nc.scalar.dma_start(
+                scale_pool[32 * quad : 32 * quad + 4, :].bitcast(I32),
+                keys_scales[0, 4 * quad : 4 * quad + 4, :].bitcast(I32),
+            )
+        nc.sync.dma_start(users3[:], planes[:, 3, :])
+        nc.sync.dma_start(word_pool[:].bitcast(I32), keys_words[0].bitcast(I32))
+        nc.sync.dma_start(place_list[:], offs4)
+
+        placed = held.tile([P, M], F32, name="placed")
+        nc.vector.memset(placed[:], 0.0)
+        ones = held.tile([P, HALF], F32, name="ones")
+        nc.scalar.activation(ones[:], placed[:, 0:HALF], ACT.Copy, bias=1.0)
+
+        key_scales = held.tile([P, I], U8, name="key_scales", align_bytes=64)
+        nc.vector.tensor_copy(key_scales[:], scale_pool[:].indirect(key_list[:]))
+
+        first = held.tile([P, PACK, Q], F32, name="first")
+        second = held.tile([P, PACK, Q], F32, name="second")
+        windows = [users012[:, 0, :], users012[:, 1, :], users012[:, 2, :], users3[:]]
+        for t in range(PACK):
+            nc.vector.tensor_copy(first[:, t, :], windows[t].indirect(first_list[:]))
+            nc.scalar.activation(second[:, t, :], windows[t].indirect(second_list[:]), ACT.Copy)
+
+        fade_col = held.tile([P, 1], F32, name="fade_col", tag="slot_a")
+        nc.sync.dma_start(fade_col[:], fade)
+        old_lo = held.tile([P, M // 2], F32, name="old_lo", tag="slot_b")
+        nc.sync.dma_start(old_lo[:], old[:, 0 : M // 2])
+
+        zq = held.tile([P, Q, PACK], BF16, name="zq", align_bytes=64)
+        nc.vector.tensor_tensor(
+            zq[:].rearrange("p (c i) t -> p c t i", i=2),
+            first[:].rearrange("p t (c i) -> p c t i", i=2),
+            second[:].rearrange("p t (c i) -> p c t i", i=2),
+            ALU.max,
+        )
+        zq_codes = held.tile([P, Q], U32, name="zq_codes", align_bytes=64)
+        zq_scales = held.tile([P, Q], U8, name="zq_scales", align_bytes=64)
+        nc.vector.quantize_mx(zq_codes[:].bitcast(FP8X4), zq_scales[:], zq[:].rearrange("p q t -> p (q t)"))
+
+        for h in range(2):
+            slots = slice(h * HALF, (h + 1) * HALF)
+            cols = slice(h * HALF // LANES, (h + 1) * HALF // LANES)
+            key_words = held.tile([P, HALF], U16, name="key_words%d" % h, align_bytes=64)
+            nc.vector.tensor_copy(key_words[:], word_pool[:].indirect(key_list[:, cols]))
+            scores = psum.tile([P, HALF], F32, name="scores%d" % h)
+            nc.tensor.matmul_mx(
+                scores[:],
+                lhsT=zq_codes[:].bitcast(FP8X4),
+                lhsT_scale=zq_scales[:],
+                rhs=key_words[:].bitcast(FP4X4),
+                rhs_scale=key_scales[:, slots],
+                start=True,
+                stop=True,
+            )
+            weights = held.tile([P, HALF], F32, name="weights%d" % h)
+            nc.scalar.activation(weights[:], scores[:], ACT.Tanh, scale=0.5)
+            nc.vector.tensor_tensor(placed[:].indirect(place_list[:, cols]), weights[:], ones[:], ALU.add)
+
+        old_hi = held.tile([P, M // 2], F32, name="old_hi", tag="slot_c")
+        nc.sync.dma_start(old_hi[:], old[:, M // 2 : M])
+        old_parts = [old_lo, old_hi]
+
+        start = 0
+        for n, width in enumerate(OUT_CHUNKS):
+            part, inside = divmod(start, M // 2)
+            result = held.tile([P, width], F32, name="result%d" % n)
+            nc.vector.scalar_tensor_tensor(
+                result[:],
+                old_parts[part][:, inside : inside + width],
+                fade_col[:],
+                placed[:, start : start + width],
+                ALU.mult,
+                ALU.add,
+            )
+            nc.sync.dma_start(out[:, start : start + width], result[:])
+            start = start + width

@@ -16,7 +16,8 @@ P = 128
 PACK = 4
 LANES = 16
 HALF = I // 2
-OUT_CHUNKS = (512, 512, 512, 256, 256)
+VECTOR_SLOTS = 128
+OUT_CHUNKS = (256, 256, 512, 512, 512)
 
 FLOPS = 2 * D * Q * I
 
@@ -36,43 +37,49 @@ def tile_attend_querylarger_counts_lean_kernel(tc, users, keys_words, keys_scale
         scale_pool = held.tile([P, T], U8, name="scale_pool")
         nc.vector.memset(scale_pool[:].bitcast(I32), 0)
 
+        planes = users.rearrange("(p t) u -> p t u", t=PACK)
+        users01 = held.tile([P, 2, U], F32, name="users01", tag="slot_a")
+        users2 = held.tile([P, U], F32, name="users2", tag="slot_b")
+        users3 = held.tile([P, U], F32, name="users3")
+        word_pool = held.tile([P, T], U16, name="word_pool")
+        nc.sync.dma_start(key_list[:], offs)
+        nc.sync.dma_start(users01[:], planes[:, 0:2, :])
+        nc.scalar.dma_start(scale_pool[0:P:8, :].bitcast(I32), keys_scales[0].bitcast(I32))
         nc.sync.dma_start(first_list[:], offs2)
         nc.sync.dma_start(second_list[:], offs3)
-        nc.sync.dma_start(key_list[:], offs)
-
-        planes = users.rearrange("(p t) u -> p t u", t=PACK)
-        users012 = held.tile([P, 3, U], F32, name="users012", tag="slot_a")
-        users3 = held.tile([P, U], F32, name="users3", tag="slot_b")
-        word_pool = held.tile([P, T], U16, name="word_pool", tag="slot_c")
-        nc.sync.dma_start(users012[:], planes[:, 0:3, :])
-        for quad in range(4):
-            nc.scalar.dma_start(
-                scale_pool[32 * quad : 32 * quad + 4, :].bitcast(I32),
-                keys_scales[0, 4 * quad : 4 * quad + 4, :].bitcast(I32),
-            )
+        nc.sync.dma_start(users2[:], planes[:, 2, :])
         nc.sync.dma_start(users3[:], planes[:, 3, :])
         nc.sync.dma_start(word_pool[:].bitcast(I32), keys_words[0].bitcast(I32))
         nc.sync.dma_start(place_list[:], offs4)
 
-        placed = held.tile([P, M], F32, name="placed")
-        nc.vector.memset(placed[:], 0.0)
-        ones = held.tile([P, HALF], F32, name="ones")
-        nc.scalar.activation(ones[:], placed[:, 0:HALF], ACT.Copy, bias=1.0)
+        placed_v = held.tile([P, M], F32, name="placed_v")
+        nc.vector.memset(placed_v[:].bitcast(I32), 0)
+        placed_s = held.tile([P, M], F32, name="placed_s")
+        nc.vector.memset(placed_s[:].bitcast(I32), 0)
+        ones = held.tile([P, VECTOR_SLOTS], F32, name="ones")
+        nc.scalar.activation(ones[:], placed_v[:, 0:VECTOR_SLOTS], ACT.Copy, bias=1.0)
 
-        key_scales = held.tile([P, I], U8, name="key_scales", align_bytes=64)
-        nc.vector.tensor_copy(key_scales[:], scale_pool[:].indirect(key_list[:]))
-
-        first = held.tile([P, PACK, Q], F32, name="first")
-        second = held.tile([P, PACK, Q], F32, name="second")
-        windows = [users012[:, 0, :], users012[:, 1, :], users012[:, 2, :], users3[:]]
+        first = held.tile([P, PACK, Q], F32, name="first", tag="slot_c", align_bytes=64)
+        second = held.tile([P, PACK, Q], F32, name="second", tag="slot_d", align_bytes=64)
+        windows = [users01[:, 0, :], users01[:, 1, :], users2[:], users3[:]]
+        nc.scalar.activation(first[:, 0, :], windows[0].indirect(first_list[:]), ACT.Copy)
         for t in range(PACK):
-            nc.vector.tensor_copy(first[:, t, :], windows[t].indirect(first_list[:]))
             nc.scalar.activation(second[:, t, :], windows[t].indirect(second_list[:]), ACT.Copy)
+
+        picked_scales = held.tile([P, I], U8, name="picked_scales")
+        nc.vector.tensor_copy(picked_scales[:], scale_pool[:].indirect(key_list[:]))
+        key_scales = held.tile([P, I], U8, name="key_scales", align_bytes=64)
+        nc.vector.tensor_copy(key_scales[:].bitcast(I32), picked_scales[:].bitcast(I32))
+        for r in range(1, 4):
+            nc.sync.dma_start(key_scales[r:P:32, :].bitcast(I32), picked_scales[8 * r : P : 32, :].bitcast(I32))
+
+        for t in range(1, PACK):
+            nc.vector.tensor_copy(first[:, t, :], windows[t].indirect(first_list[:]))
 
         fade_col = held.tile([P, 1], F32, name="fade_col", tag="slot_a")
         nc.sync.dma_start(fade_col[:], fade)
-        old_lo = held.tile([P, M // 2], F32, name="old_lo", tag="slot_b")
-        nc.sync.dma_start(old_lo[:], old[:, 0 : M // 2])
+        old_sb = held.tile([P, M], F32, name="old_sb", tag="slot_b")
+        nc.sync.dma_start(old_sb[:], old)
 
         zq = held.tile([P, Q, PACK], BF16, name="zq", align_bytes=64)
         nc.vector.tensor_tensor(
@@ -81,44 +88,46 @@ def tile_attend_querylarger_counts_lean_kernel(tc, users, keys_words, keys_scale
             second[:].rearrange("p t (c i) -> p c t i", i=2),
             ALU.max,
         )
+        words_lo = held.tile([P, HALF], U16, name="words_lo", tag="slot_c", align_bytes=64)
+        words_hi = held.tile([P, HALF], U16, name="words_hi", tag="slot_d", align_bytes=64)
         zq_codes = held.tile([P, Q], U32, name="zq_codes", align_bytes=64)
         zq_scales = held.tile([P, Q], U8, name="zq_scales", align_bytes=64)
         nc.vector.quantize_mx(zq_codes[:].bitcast(FP8X4), zq_scales[:], zq[:].rearrange("p q t -> p (q t)"))
+        nc.vector.tensor_copy(words_lo[:], word_pool[:].indirect(key_list[:, 0 : HALF // LANES]))
+        nc.vector.tensor_copy(words_hi[:], word_pool[:].indirect(key_list[:, HALF // LANES : I // LANES]))
 
-        for h in range(2):
-            slots = slice(h * HALF, (h + 1) * HALF)
-            cols = slice(h * HALF // LANES, (h + 1) * HALF // LANES)
-            key_words = held.tile([P, HALF], U16, name="key_words%d" % h, align_bytes=64)
-            nc.vector.tensor_copy(key_words[:], word_pool[:].indirect(key_list[:, cols]))
-            scores = psum.tile([P, HALF], F32, name="scores%d" % h)
+        halves = held.tile([P, I], F32, name="halves")
+        pieces = [
+            (0, VECTOR_SLOTS, words_lo[:, 0:VECTOR_SLOTS]),
+            (VECTOR_SLOTS, HALF, words_lo[:, VECTOR_SLOTS:HALF]),
+            (HALF, I, words_hi[:]),
+        ]
+        for lo, hi, words in pieces:
+            scores = psum.tile([P, hi - lo], F32, name="scores%d" % lo)
             nc.tensor.matmul_mx(
                 scores[:],
                 lhsT=zq_codes[:].bitcast(FP8X4),
                 lhsT_scale=zq_scales[:],
-                rhs=key_words[:].bitcast(FP4X4),
-                rhs_scale=key_scales[:, slots],
+                rhs=words.bitcast(FP4X4),
+                rhs_scale=key_scales[:, lo:hi],
                 start=True,
                 stop=True,
             )
-            weights = held.tile([P, HALF], F32, name="weights%d" % h)
-            nc.scalar.activation(weights[:], scores[:], ACT.Tanh, scale=0.5)
-            nc.vector.tensor_tensor(placed[:].indirect(place_list[:, cols]), weights[:], ones[:], ALU.add)
+            nc.scalar.activation(halves[:, lo:hi], scores[:], ACT.Tanh, scale=0.5)
 
-        old_hi = held.tile([P, M // 2], F32, name="old_hi", tag="slot_c")
-        nc.sync.dma_start(old_hi[:], old[:, M // 2 : M])
-        old_parts = [old_lo, old_hi]
+        nc.vector.tensor_tensor(
+            placed_v[:].indirect(place_list[:, 0 : VECTOR_SLOTS // LANES]), halves[:, 0:VECTOR_SLOTS], ones[:], ALU.add
+        )
+        nc.scalar.activation(
+            placed_s[:].indirect(place_list[:, VECTOR_SLOTS // LANES : I // LANES]), halves[:, VECTOR_SLOTS:I], ACT.Copy, bias=1.0
+        )
+
+        partial = held.tile([P, M], F32, name="partial")
+        nc.vector.scalar_tensor_tensor(partial[:], old_sb[:], fade_col[:], placed_v[:], ALU.mult, ALU.add)
 
         start = 0
         for n, width in enumerate(OUT_CHUNKS):
-            part, inside = divmod(start, M // 2)
             result = held.tile([P, width], F32, name="result%d" % n)
-            nc.vector.scalar_tensor_tensor(
-                result[:],
-                old_parts[part][:, inside : inside + width],
-                fade_col[:],
-                placed[:, start : start + width],
-                ALU.mult,
-                ALU.add,
-            )
+            nc.vector.tensor_tensor(result[:], partial[:, start : start + width], placed_s[:, start : start + width], ALU.add)
             nc.sync.dma_start(out[:, start : start + width], result[:])
             start = start + width

@@ -17,7 +17,8 @@ PACK = 4
 LANES = 16
 HALF = I // 2
 VECTOR_SLOTS = 128
-OUT_CHUNKS = (256, 256, 512, 512, 512)
+OUT_HALVES = (slice(0, M // 2), slice(M // 2, M))
+OUT_CHUNKS = (256, 256, 512, 512, 256, 256)
 
 FLOPS = 2 * D * Q * I
 
@@ -38,11 +39,13 @@ def tile_attend_querylarger_counts_lean_kernel(tc, users, keys_words, keys_scale
         nc.vector.memset(scale_pool[:].bitcast(I32), 0)
 
         planes = users.rearrange("(p t) u -> p t u", t=PACK)
-        users01 = held.tile([P, 2, U], F32, name="users01", tag="slot_a")
+        users01 = held.tile([P, 2, U], F32, name="users01")
         users2 = held.tile([P, U], F32, name="users2", tag="slot_b")
         users3 = held.tile([P, U], F32, name="users3")
         word_pool = held.tile([P, T], U16, name="word_pool")
+        fade_col = held.tile([P, 1], F32, name="fade_col")
         nc.sync.dma_start(key_list[:], offs)
+        nc.scalar.dma_start(fade_col[:], fade)
         nc.sync.dma_start(users01[:], planes[:, 0:2, :])
         nc.scalar.dma_start(scale_pool[0:P:8, :].bitcast(I32), keys_scales[0].bitcast(I32))
         nc.sync.dma_start(first_list[:], offs2)
@@ -76,10 +79,9 @@ def tile_attend_querylarger_counts_lean_kernel(tc, users, keys_words, keys_scale
         for t in range(1, PACK):
             nc.vector.tensor_copy(first[:, t, :], windows[t].indirect(first_list[:]))
 
-        fade_col = held.tile([P, 1], F32, name="fade_col", tag="slot_a")
-        nc.sync.dma_start(fade_col[:], fade)
         old_sb = held.tile([P, M], F32, name="old_sb", tag="slot_b")
-        nc.sync.dma_start(old_sb[:], old)
+        for cols in OUT_HALVES:
+            nc.sync.dma_start(old_sb[:, cols], old[:, cols])
 
         zq = held.tile([P, Q, PACK], BF16, name="zq", align_bytes=64)
         nc.vector.tensor_tensor(
@@ -123,7 +125,8 @@ def tile_attend_querylarger_counts_lean_kernel(tc, users, keys_words, keys_scale
         )
 
         partial = held.tile([P, M], F32, name="partial")
-        nc.vector.scalar_tensor_tensor(partial[:], old_sb[:], fade_col[:], placed_v[:], ALU.mult, ALU.add)
+        for cols in OUT_HALVES:
+            nc.vector.scalar_tensor_tensor(partial[:, cols], old_sb[:, cols], fade_col[:], placed_v[:, cols], ALU.mult, ALU.add)
 
         start = 0
         for n, width in enumerate(OUT_CHUNKS):

@@ -39,17 +39,15 @@ def tile_attend_querylarger_counts_lean_kernel(tc, users, keys_words, keys_scale
         nc.vector.memset(scale_pool[:].bitcast(I32), 0)
 
         planes = users.rearrange("(p t) u -> p t u", t=PACK)
-        users01 = held.tile([P, 2, U], F32, name="users01")
-        users2 = held.tile([P, U], F32, name="users2", tag="slot_b")
-        users3 = held.tile([P, U], F32, name="users3")
+        users01 = held.tile([P, 2, U], F32, name="users01", tag="slot_a")
+        users2 = held.tile([P, U], F32, name="users2")
+        users3 = held.tile([P, U], F32, name="users3", tag="slot_b")
         word_pool = held.tile([P, T], U16, name="word_pool")
-        fade_col = held.tile([P, 1], F32, name="fade_col")
-        nc.sync.dma_start(key_list[:], offs)
-        nc.scalar.dma_start(fade_col[:], fade)
         nc.sync.dma_start(users01[:], planes[:, 0:2, :])
         nc.scalar.dma_start(scale_pool[0:P:8, :].bitcast(I32), keys_scales[0].bitcast(I32))
         nc.sync.dma_start(first_list[:], offs2)
         nc.sync.dma_start(second_list[:], offs3)
+        nc.sync.dma_start(key_list[:], offs)
         nc.sync.dma_start(users2[:], planes[:, 2, :])
         nc.sync.dma_start(users3[:], planes[:, 3, :])
         nc.sync.dma_start(word_pool[:].bitcast(I32), keys_words[0].bitcast(I32))
@@ -65,9 +63,12 @@ def tile_attend_querylarger_counts_lean_kernel(tc, users, keys_words, keys_scale
         first = held.tile([P, PACK, Q], F32, name="first", tag="slot_c", align_bytes=64)
         second = held.tile([P, PACK, Q], F32, name="second", tag="slot_d", align_bytes=64)
         windows = [users01[:, 0, :], users01[:, 1, :], users2[:], users3[:]]
-        nc.scalar.activation(first[:, 0, :], windows[0].indirect(first_list[:]), ACT.Copy)
         for t in range(PACK):
+            if t == 2:
+                nc.scalar.activation(first[:, t, :], windows[t].indirect(first_list[:]), ACT.Copy)
             nc.scalar.activation(second[:, t, :], windows[t].indirect(second_list[:]), ACT.Copy)
+        for t in range(2):
+            nc.vector.tensor_copy(first[:, t, :], windows[t].indirect(first_list[:]))
 
         picked_scales = held.tile([P, I], U8, name="picked_scales")
         nc.vector.tensor_copy(picked_scales[:], scale_pool[:].indirect(key_list[:]))
@@ -76,9 +77,10 @@ def tile_attend_querylarger_counts_lean_kernel(tc, users, keys_words, keys_scale
         for r in range(1, 4):
             nc.sync.dma_start(key_scales[r:P:32, :].bitcast(I32), picked_scales[8 * r : P : 32, :].bitcast(I32))
 
-        for t in range(1, PACK):
-            nc.vector.tensor_copy(first[:, t, :], windows[t].indirect(first_list[:]))
+        nc.vector.tensor_copy(first[:, 3, :], windows[3].indirect(first_list[:]))
 
+        fade_col = held.tile([P, 1], F32, name="fade_col", tag="slot_a")
+        nc.sync.dma_start(fade_col[:], fade)
         old_sb = held.tile([P, M], F32, name="old_sb", tag="slot_b")
         for cols in OUT_HALVES:
             nc.sync.dma_start(old_sb[:, cols], old[:, cols])

import concourse.mybir as mybir

F32 = mybir.dt.float32
BF16 = mybir.dt.bfloat16
I32 = mybir.dt.int32
U32 = mybir.dt.uint32
U16 = mybir.dt.uint16
U8 = mybir.dt.uint8
FP8X4 = mybir.dt.float8_e4m3fn_x4
FP4X4 = mybir.dt.float4_e2m1fn_x4
ALU = mybir.AluOpType
ACT = mybir.ActivationFunctionType

D, T, I, Q, U, M = 512, 2048, 512, 128, 1024, 2048
P = 128
PACK = 4
LANES = 16
HALF = I // 2
VECTOR_SLOTS = 128
OUT_HALVES = (slice(0, M // 2), slice(M // 2, M))
OUT_CHUNKS = (256, 256, 512, 512, 256, 256)

FLOPS = 2 * D * Q * I


def tile_attend_querylarger_counts_lean_kernel(tc, users, keys_words, keys_scales, old, fade, offs, offs2, offs3, offs4, out):
    nc = tc.nc
    with (
        tc.tile_pool(name="lists", bufs=1) as lists,
        tc.tile_pool(name="held", bufs=1) as held,
        tc.psum_pool(name="psum", bufs=1) as psum,
    ):
        key_list = lists.tile([P, I // LANES], U16, name="key_list")
        first_list = lists.tile([P, Q // LANES], U16, name="first_list")
        second_list = lists.tile([P, Q // LANES], U16, name="second_list")
        place_list = lists.tile([P, I // LANES], U16, name="place_list")

        scale_pool = held.tile([P, T], U8, name="scale_pool")
        nc.vector.memset(scale_pool[:].bitcast(I32), 0)

        planes = users.rearrange("(p t) u -> p t u", t=PACK)
        users01 = held.tile([P, 2, U], F32, name="users01", tag="slot_a")
        users2 = held.tile([P, U], F32, name="users2")
        users3 = held.tile([P, U], F32, name="users3", tag="slot_b")
        word_pool = held.tile([P, T], U16, name="word_pool")
        nc.sync.dma_start(users01[:], planes[:, 0:2, :])
        nc.scalar.dma_start(scale_pool[0:P:8, :].bitcast(I32), keys_scales[0].bitcast(I32))
        nc.sync.dma_start(first_list[:], offs2)
        nc.sync.dma_start(second_list[:], offs3)
        nc.sync.dma_start(key_list[:], offs)
        nc.sync.dma_start(users2[:], planes[:, 2, :])
        nc.sync.dma_start(users3[:], planes[:, 3, :])
        nc.sync.dma_start(word_pool[:].bitcast(I32), keys_words[0].bitcast(I32))
        nc.sync.dma_start(place_list[:], offs4)

        placed_v = held.tile([P, M], F32, name="placed_v")
        nc.vector.memset(placed_v[:].bitcast(I32), 0)
        placed_s = held.tile([P, M], F32, name="placed_s")
        nc.vector.memset(placed_s[:].bitcast(I32), 0)
        ones = held.tile([P, VECTOR_SLOTS], F32, name="ones")
        nc.scalar.activation(ones[:], placed_v[:, 0:VECTOR_SLOTS], ACT.Copy, bias=1.0)

        first = held.tile([P, PACK, Q], F32, name="first", tag="slot_c", align_bytes=64)
        second = held.tile([P, PACK, Q], F32, name="second", tag="slot_d", align_bytes=64)
        windows = [users01[:, 0, :], users01[:, 1, :], users2[:], users3[:]]
        for t in range(PACK):
            if t == 2:
                nc.scalar.activation(first[:, t, :], windows[t].indirect(first_list[:]), ACT.Copy)
            nc.scalar.activation(second[:, t, :], windows[t].indirect(second_list[:]), ACT.Copy)
        for t in range(2):
            nc.vector.tensor_copy(first[:, t, :], windows[t].indirect(first_list[:]))

        picked_scales = held.tile([P, I], U8, name="picked_scales")
        nc.vector.tensor_copy(picked_scales[:], scale_pool[:].indirect(key_list[:]))
        key_scales = held.tile([P, I], U8, name="key_scales", align_bytes=64)
        nc.vector.tensor_copy(key_scales[:].bitcast(I32), picked_scales[:].bitcast(I32))
        for r in range(1, 4):
            nc.sync.dma_start(key_scales[r:P:32, :].bitcast(I32), picked_scales[8 * r : P : 32, :].bitcast(I32))

        nc.vector.tensor_copy(first[:, 3, :], windows[3].indirect(first_list[:]))

        fade_col = held.tile([P, 1], F32, name="fade_col", tag="slot_a")
        nc.sync.dma_start(fade_col[:], fade)
        old_sb = held.tile([P, M], F32, name="old_sb", tag="slot_b")
        for cols in OUT_HALVES:
            nc.sync.dma_start(old_sb[:, cols], old[:, cols])

        zq = held.tile([P, Q, PACK], BF16, name="zq", align_bytes=64)
        nc.vector.tensor_tensor(
            zq[:].rearrange("p (c i) t -> p c t i", i=2),
            first[:].rearrange("p t (c i) -> p c t i", i=2),
            second[:].rearrange("p t (c i) -> p c t i", i=2),
            ALU.max,
        )
        words_lo = held.tile([P, HALF], U16, name="words_lo", tag="slot_c", align_bytes=64)
        words_hi = held.tile([P, HALF], U16, name="words_hi", tag="slot_d", align_bytes=64)
        zq_codes = held.tile([P, Q], U32, name="zq_codes", align_bytes=64)
        zq_scales = held.tile([P, Q], U8, name="zq_scales", align_bytes=64)
        nc.vector.quantize_mx(zq_codes[:].bitcast(FP8X4), zq_scales[:], zq[:].rearrange("p q t -> p (q t)"))
        nc.vector.tensor_copy(words_lo[:], word_pool[:].indirect(key_list[:, 0 : HALF // LANES]))
        nc.vector.tensor_copy(words_hi[:], word_pool[:].indirect(key_list[:, HALF // LANES : I // LANES]))

        halves = held.tile([P, I], F32, name="halves")
        pieces = [
            (0, VECTOR_SLOTS, words_lo[:, 0:VECTOR_SLOTS]),
            (VECTOR_SLOTS, HALF, words_lo[:, VECTOR_SLOTS:HALF]),
            (HALF, I, words_hi[:]),
        ]
        for lo, hi, words in pieces:
            scores = psum.tile([P, hi - lo], F32, name="scores%d" % lo)
            nc.tensor.matmul_mx(
                scores[:],
                lhsT=zq_codes[:].bitcast(FP8X4),
                lhsT_scale=zq_scales[:],
                rhs=words.bitcast(FP4X4),
                rhs_scale=key_scales[:, lo:hi],
                start=True,
                stop=True,
            )
            nc.scalar.activation(halves[:, lo:hi], scores[:], ACT.Tanh, scale=0.5)

        nc.vector.tensor_tensor(
            placed_v[:].indirect(place_list[:, 0 : VECTOR_SLOTS // LANES]), halves[:, 0:VECTOR_SLOTS], ones[:], ALU.add
        )
        nc.scalar.activation(
            placed_s[:].indirect(place_list[:, VECTOR_SLOTS // LANES : I // LANES]), halves[:, VECTOR_SLOTS:I], ACT.Copy, bias=1.0
        )

        partial = held.tile([P, M], F32, name="partial")
        for cols in OUT_HALVES:
            nc.vector.scalar_tensor_tensor(partial[:, cols], old_sb[:, cols], fade_col[:], placed_v[:, cols], ALU.mult, ALU.add)

        start = 0
        for n, width in enumerate(OUT_CHUNKS):
            result = held.tile([P, width], F32, name="result%d" % n)
            nc.vector.tensor_tensor(result[:], partial[:, start : start + width], placed_s[:, start : start + width], ALU.add)
            nc.sync.dma_start(out[:, start : start + width], result[:])
            start = start + width
